import numpy as np, ml_dtypes
CORES = [35,38,43,46]
N = 4
VB, TK = 4, 128
def setup_inputs(rng):
    h = rng.standard_normal((128, TK), dtype=np.float32) / 4; w = rng.standard_normal((N, 128, VB * 128), dtype=np.float32)
    a = 2 * np.pi * rng.random((TK)); s = 400 * rng.random((TK)) ** 1.5; h[0] = s * np.cos(a); h[1] = s * np.sin(a); h[2] = 150 * rng.standard_normal((TK)); w[:, 2, :] = 1 + w[:, 2, :] / 50
    a = (2 * np.pi * rng.random() + np.pi / 2 * (rng.permutation(N).reshape(N, 1, 1) + 0.5) / N - 0.5 + (np.arange(VB).reshape(1, VB, 1) + rng.random((N, VB, 128))) / VB).reshape(N, VB * 128); w[:, 0, :] = np.cos(a); w[:, 1, :] = np.sin(a)
    tgt = rng.integers(0, N * VB * 128, size=TK)
    oh = np.zeros((N * VB * 128, TK), np.float32); oh[tgt, np.arange(TK)] = 1.0
    oh = oh.reshape(N, VB, 128, TK).transpose(0, 2, 1, 3).reshape(N, 128, VB * TK)
    return {"h": np.broadcast_to(h, (N, 128, TK)).astype(ml_dtypes.bfloat16), "w": w.astype(ml_dtypes.bfloat16), "oh": oh.astype(ml_dtypes.bfloat16)}
def reference(h, w, oh):
    H, W, OH = h.astype(np.float64), w.astype(np.float64), oh.astype(np.float64)
    Z = np.concatenate([W[r].T @ H[r] for r in range(N)], axis=0)
    O = np.concatenate([OH[r][:, TK * b:TK * b + TK] for r in range(N) for b in range(VB)], axis=0)
    m = Z.max(axis=0)
    l = m + np.log(np.exp(Z - m).sum(axis=0)) - (O * Z).sum(axis=0)
    return {"l": np.broadcast_to(l.astype(np.float32), (N, 1, TK))}

@@ -1,0 +1,197 @@
+import math
+from concourse.bass import DstId, RemoteDMATransfer
+from concourse.mybir import AluOpType, AxisListType, ActivationFunctionType
+
+VB, TK, NR = 4, 128, 4
+KINDS = 3
+SLOT = VB * KINDS
+BIG = 2048.0
+Q = 16
+J = 128
+D = math.log(1.0 + 1.0 / Q)
+_R = 1.0 / (Q * D)
+HALF_GAP = (math.log(_R) - D * Q * (_R - 1.0)) / 2.0
+
+SCRATCH = {
+    "hs": ("sbuf", [128, TK], "bfloat16"),
+    "ws": ("sbuf", [128, VB * 128], "bfloat16"),
+    "ohs": ("sbuf", [128, VB * TK], "bfloat16"),
+    "eye": ("sbuf", [128, 128], "bfloat16"),
+    "jt": ("sbuf", [128, J], "float32"),
+    "cap": ("sbuf", [128, J], "float32"),
+    "ptab": ("sbuf", [128, J], "float32"),
+    "ex": ("sbuf", [128, VB * 128], "float32"),
+    "stat": ("sbuf", [128, NR * SLOT], "float32"),
+    "fac": ("sbuf", [128, NR * VB], "float32"),
+    "fs": ("sbuf", [128, NR * VB], "float32"),
+    "xs": ("sbuf", [128, J], "float32"),
+    "ys": ("sbuf", [128, J], "float32"),
+    "sc": ("sbuf", [128, 8], "float32"),
+}
+for _b in range(VB):
+    SCRATCH["za%d" % _b] = ("psum", [128, 512], "float32")
+    SCRATCH["zb%d" % _b] = ("psum", [128, 512], "float32")
+
+SEMAPHORES = ["ld_h", "ld_w", "ld_oh", "fill", "io_j", "diag", "io_c", "tab", "arr", "sent",
+              "v1", "e1", "v2", "v3", "v4", "v5", "vg1", "vg2", "v6", "stored"]
+for _b in range(VB):
+    SEMAPHORES += ["za%d" % _b, "zb%d" % _b, "nm%d" % _b, "sm%d" % _b, "gq%d" % _b]
+
+
+def _bits(mask):
+    return [1 << i for i in range(mask.bit_length()) if (mask >> i) & 1]
+
+
+def _join(bits):
+    m = 0
+    for x in bits:
+        m |= x
+    return m
+
+
+def _pow2(n):
+    p = 1
+    while p * 2 <= n:
+        p *= 2
+    return p
+
+
+def _plan(core, cores, topo):
+    peers = [c for c in cores if c != core]
+    near = [c for c in peers if topo.chip(c) == topo.chip(core)]
+    far = [c for c in peers if topo.chip(c) != topo.chip(core)]
+    leave = topo.mask(core, far[0])
+    for c in far:
+        leave &= topo.mask(core, c)
+    lb = _bits(leave)
+    n = _pow2(len(lb) // len(far))
+    fmask = {c: _join(lb[i * n:(i + 1) * n]) for i, c in enumerate(far)}
+    stay = _bits(topo.mask(core, near[0]) & ~leave)
+    smask = _join(stay[:_pow2(len(stay))])
+    return near, far, fmask, smask
+
+
+def _count(mask):
+    return len(_bits(mask))
+
+
+def rank_program(g, core, T, topo):
+    rank = T.rank_of(core)
+    if rank is None:
+        return
+    S = T.sem
+    X = AxisListType.X
+    EXP = ActivationFunctionType.Exp
+    A = AluOpType
+    base = rank * SLOT
+    stat = T.stat
+
+    def col(b, k):
+        c = base + KINDS * b + k
+        return stat[:, c:c + 1]
+
+    def blk(t, b):
+        return t[:, 128 * b:128 * b + 128]
+
+    g.sync.dma_start(T.ws[:], T.w[:]).then_inc(S.ld_w, 16)
+    g.scalar.dma_start(T.hs[:], T.h[:]).then_inc(S.ld_h, 16)
+    g.sync.dma_start(T.ohs[:], T.oh[:]).then_inc(S.ld_oh, 16)
+
+    g.vector.memset(T.eye[:], BIG).then_inc(S.fill, 1)
+    g.iota(T.jt[:], [[1, J]], 0, 0, allow_small_or_imprecise_dtypes=True).then_inc(S.io_j, 1)
+    g.wait_ge(S.fill, 1)
+    g.affine_select(T.eye[:], T.eye[:], [[-1, 128]], A.is_equal, 0.0, 0, 1).then_inc(S.diag, 1)
+    g.iota(T.cap[:], [[Q + 1, J]], Q + 1 - J * Q, 0, allow_small_or_imprecise_dtypes=True).then_inc(S.io_c, 1)
+    g.scalar.wait_ge(S.io_j, 1)
+    g.scalar.activation(T.ptab[:], T.jt[:], EXP, bias=math.log(Q) + HALF_GAP, scale=-D).then_inc(S.tab, 1)
+
+    g.tensor.wait_ge(S.ld_h, 16)
+    g.tensor.wait_ge(S.ld_w, 16)
+    for b in range(VB):
+        g.tensor.matmul(T["za%d" % b][:, 0:128], T.hs[:], blk(T.ws, b), True, True).then_inc(S["za%d" % b], 1)
+    for b in range(VB):
+        g.tensor.matmul(T["zb%d" % b][:, 0:128], T.hs[:], blk(T.ws, b), True, False)
+    g.tensor.wait_ge(S.ld_oh, 16)
+    g.tensor.wait_ge(S.diag, 1)
+    for b in range(VB):
+        g.tensor.matmul(T["zb%d" % b][:, 0:128], blk(T.ohs, b), T.eye[:], False, True).then_inc(S["zb%d" % b], 1)
+
+    for b in range(VB):
+        g.vector.wait_ge(S["za%d" % b], 1)
+        g.vector.tensor_reduce(col(b, 0), T["za%d" % b][:, 0:128], X, A.max, negate=True).then_inc(S["nm%d" % b], 1)
+        g.scalar.wait_ge(S["nm%d" % b], 1)
+        g.scalar.activation(blk(T.ex, b), T["za%d" % b][:, 0:128], EXP, bias=col(b, 0), scale=1.0,
+                            accum_out=col(b, 1)).then_inc(S["sm%d" % b], 1)
+    for b in range(VB):
+        g.vector.wait_ge(S["zb%d" % b], 1)
+        g.vector.tensor_reduce(col(b, 2), T["zb%d" % b][:, 0:128], X, A.max).then_inc(S["gq%d" % b], 1)
+
+    near, far, fmask, smask = _plan(core, T.cores, topo)
+    nb = near[0]
+    rid, pid, _ = topo.addr(nb)
+    early = topo.mask(core, nb)
+    head = stat[:, base:base + 2]
+    tail = stat[:, base + 2:base + SLOT]
+    slot = stat[:, base:base + SLOT]
+    g.wait_ge(S.nm0, 1)
+    g.wait_ge(S.sm0, 1)
+    g.remote_dma(head, head, S.arr, S.sent, pid, rid, early)
+    for b in range(VB):
+        g.wait_ge(S["nm%d" % b], 1)
+        g.wait_ge(S["sm%d" % b], 1)
+    for b in range(VB):
+        g.wait_ge(S["gq%d" % b], 1)
+    trs = []
+    for c in far:
+        r2, p2, _ = topo.addr(c)
+        trs.append(RemoteDMATransfer(dst_ids=[DstId(rid=r2, pnc=p2)], dma_engine_mask=fmask[c], remote_sem=S.arr,
+                                     src=slot, dst=slot))
+    g.remote_dma_fused(trs, local_sem=S.sent)
+    g.remote_dma(tail, tail, S.arr, S.sent, pid, rid, smask)
+    sent = _count(early) + _count(smask) + sum(_count(fmask[c]) for c in far)
+    arrive = 0
+    for c in T.cores:
+        if c == core:
+            continue
+        n2, f2, fm2, sm2 = _plan(c, T.cores, topo)
+        if core in n2:
+            arrive += _count(topo.mask(c, core)) + _count(sm2)
+        else:
+            arrive += _count(fm2[core])
+
+    nms = stat[:, 0:NR * SLOT:KINDS]
+    sms = stat[:, 1:NR * SLOT:KINDS]
+    gqs = stat[:, 2:NR * SLOT:KINDS]
+    NM, SS, NG, BB, LL = (T.sc[:, k:k + 1] for k in range(5))
+    v = g.vector
+    for b in range(VB):
+        v.wait_ge(S["nm%d" % b], 1)
+        v.wait_ge(S["sm%d" % b], 1)
+        v.wait_ge(S["gq%d" % b], 1)
+    v.wait_ge(S.tab, 1)
+    v.wait_ge(S.io_c, 1)
+    v.wait_ge(S.arr, arrive)
+    v.tensor_reduce(NM, nms, X, A.min).then_inc(S.v1, 1)
+    g.scalar.wait_ge(S.arr, arrive)
+    g.scalar.wait_ge(S.v1, 1)
+    g.scalar.activation(T.fac[:], nms, EXP, bias=NM, scale=-1.0).then_inc(S.e1, 1)
+    v.tensor_reduce(NG, gqs, X, A.max, negate=True).then_inc(S.vg1, 1)
+    v.wait_ge(S.v1, 1)
+    v.wait_ge(S.vg1, 1)
+    v.tensor_scalar(BB, NG, BIG, NM, A.add, A.subtract).then_inc(S.vg2, 1)
+    v.wait_ge(S.e1, 1)
+    v.tensor_tensor(T.fs[:], T.fac[:], sms, A.mult).then_inc(S.v2, 1)
+    v.wait_ge(S.v2, 1)
+    v.tensor_reduce(SS, T.fs[:], X, A.add).then_inc(S.v3, 1)
+    v.wait_ge(S.v3, 1)
+    v.tensor_scalar(T.xs[:], T.ptab[:], SS, float(Q), A.mult, A.max).then_inc(S.v4, 1)
+    v.wait_ge(S.v4, 1)
+    v.tensor_tensor_scan(T.ys[:], T.xs[:], T.cap[:], float(-J * Q), A.add, A.min).then_inc(S.v5, 1)
+    v.wait_ge(S.v5, 1)
+    v.wait_ge(S.vg2, 1)
+    v.tensor_scalar(LL, T.ys[:, J - 1:J], D, BB, A.mult, A.add).then_inc(S.v6, 1)
+
+    g.sync.wait_ge(S.v6, 1)
+    g.sync.dma_start(T.l[:], LL).then_inc(S.stored, 16)
+    g.sync.wait_ge(S.stored, 16)
+    g.wait_ge(S.sent, sent)

@@ -27,12 +27,13 @@ SCRATCH = {
     "xs": ("sbuf", [128, J], "float32"),
     "ys": ("sbuf", [128, J], "float32"),
     "sc": ("sbuf", [128, 8], "float32"),
+    "pidx": ("sbuf", [128, 1], "float32"),
 }
 for _b in range(VB):
     SCRATCH["za%d" % _b] = ("psum", [128, 512], "float32")
     SCRATCH["zb%d" % _b] = ("psum", [128, 512], "float32")
 
-SEMAPHORES = ["ld_h", "ld_w", "ld_oh", "fill", "io_j", "diag", "io_c", "tab", "arr", "sent",
+SEMAPHORES = ["ld_h", "ld_w", "ld_oh", "io_p", "io_j", "diag", "io_c", "tab", "arr", "arrc", "sent",
               "v1", "e1", "v2", "v3", "v4", "v5", "vg1", "vg2", "v6", "stored"]
 for _b in range(VB):
     SEMAPHORES += ["za%d" % _b, "zb%d" % _b, "nm%d" % _b, "sm%d" % _b, "gq%d" % _b]
@@ -65,10 +66,12 @@ def _plan(core, cores, topo):
         leave &= topo.mask(core, c)
     lb = _bits(leave)
     n = _pow2(len(lb) // len(far))
-    fmask = {c: _join(lb[i * n:(i + 1) * n]) for i, c in enumerate(far)}
+    plan = {c: _join(lb[i * n:(i + 1) * n]) for i, c in enumerate(far)}
     stay = _bits(topo.mask(core, near[0]) & ~leave)
-    smask = _join(stay[:_pow2(len(stay))])
-    return near, far, fmask, smask
+    n = _pow2(len(stay) // len(near))
+    for i, c in enumerate(near):
+        plan[c] = _join(stay[i * n:(i + 1) * n])
+    return plan
 
 
 def _count(mask):
@@ -97,13 +100,28 @@ def rank_program(g, core, T, topo):
     g.scalar.dma_start(T.hs[:], T.h[:]).then_inc(S.ld_h, 16)
     g.sync.dma_start(T.ohs[:], T.oh[:]).then_inc(S.ld_oh, 16)
 
-    g.vector.memset(T.eye[:], BIG).then_inc(S.fill, 1)
+    home = [c for c in T.cores if topo.chip(c) == topo.chip(core)]
+    W = J // len(home)
+    k0 = home.index(core)
+    mine = T.cap[:, k0 * W:k0 * W + W]
     g.iota(T.jt[:], [[1, J]], 0, 0, allow_small_or_imprecise_dtypes=True).then_inc(S.io_j, 1)
-    g.wait_ge(S.fill, 1)
-    g.affine_select(T.eye[:], T.eye[:], [[-1, 128]], A.is_equal, 0.0, 0, 1).then_inc(S.diag, 1)
-    g.iota(T.cap[:], [[Q + 1, J]], Q + 1 - J * Q, 0, allow_small_or_imprecise_dtypes=True).then_inc(S.io_c, 1)
+    g.iota(T.pidx[:], [[0, 1]], 0, 1, allow_small_or_imprecise_dtypes=True).then_inc(S.io_p, 1)
+    g.iota(mine, [[Q + 1, W]], (Q + 1) * (1 + k0 * W) - J * Q, 0,
+           allow_small_or_imprecise_dtypes=True).then_inc(S.io_c, 1)
+    g.wait_ge(S.io_c, 1)
+    sent = 0
+    capin = 0
+    for c in home:
+        if c != core:
+            rid, pid, _ = topo.addr(c)
+            g.remote_dma(mine, mine, S.arrc, S.sent, pid, rid, topo.mask(core, c))
+            sent += _count(topo.mask(core, c))
+            capin += _count(topo.mask(c, core))
     g.scalar.wait_ge(S.io_j, 1)
     g.scalar.activation(T.ptab[:], T.jt[:], EXP, bias=math.log(Q) + HALF_GAP, scale=-D).then_inc(S.tab, 1)
+    g.vector.wait_ge(S.io_j, 1)
+    g.vector.wait_ge(S.io_p, 1)
+    g.vector.tensor_scalar(T.eye[:], T.jt[:, 0:128], T.pidx[:], BIG, A.is_equal, A.mult).then_inc(S.diag, 1)
 
     g.tensor.wait_ge(S.ld_h, 16)
     g.tensor.wait_ge(S.ld_w, 16)
@@ -126,43 +144,26 @@ def rank_program(g, core, T, topo):
         g.vector.wait_ge(S["zb%d" % b], 1)
         g.vector.tensor_reduce(col(b, 2), T["zb%d" % b][:, 0:128], X, A.max).then_inc(S["gq%d" % b], 1)
 
-    near, far, fmask, smask = _plan(core, T.cores, topo)
-    nb = near[0]
-    rid, pid, _ = topo.addr(nb)
-    early = topo.mask(core, nb)
-    head = stat[:, base:base + 2]
-    tail = stat[:, base + 2:base + SLOT]
+    plan = _plan(core, T.cores, topo)
     slot = stat[:, base:base + SLOT]
-    g.wait_ge(S.nm0, 1)
-    g.wait_ge(S.sm0, 1)
-    g.remote_dma(head, head, S.arr, S.sent, pid, rid, early)
     for b in range(VB):
         g.wait_ge(S["nm%d" % b], 1)
         g.wait_ge(S["sm%d" % b], 1)
     for b in range(VB):
         g.wait_ge(S["gq%d" % b], 1)
     trs = []
-    for c in far:
-        r2, p2, _ = topo.addr(c)
-        trs.append(RemoteDMATransfer(dst_ids=[DstId(rid=r2, pnc=p2)], dma_engine_mask=fmask[c], remote_sem=S.arr,
+    for c in plan:
+        rid, pid, _ = topo.addr(c)
+        trs.append(RemoteDMATransfer(dst_ids=[DstId(rid=rid, pnc=pid)], dma_engine_mask=plan[c], remote_sem=S.arr,
                                      src=slot, dst=slot))
     g.remote_dma_fused(trs, local_sem=S.sent)
-    g.remote_dma(tail, tail, S.arr, S.sent, pid, rid, smask)
-    sent = _count(early) + _count(smask) + sum(_count(fmask[c]) for c in far)
-    arrive = 0
-    for c in T.cores:
-        if c == core:
-            continue
-        n2, f2, fm2, sm2 = _plan(c, T.cores, topo)
-        if core in n2:
-            arrive += _count(topo.mask(c, core)) + _count(sm2)
-        else:
-            arrive += _count(fm2[core])
+    sent += sum(_count(plan[c]) for c in plan)
+    arrive = sum(_count(_plan(c, T.cores, topo)[core]) for c in T.cores if c != core)
 
     nms = stat[:, 0:NR * SLOT:KINDS]
     sms = stat[:, 1:NR * SLOT:KINDS]
     gqs = stat[:, 2:NR * SLOT:KINDS]
-    NM, SS, NG, BB, LL = (T.sc[:, k:k + 1] for k in range(5))
+    NM, SS, NG, BB, LL = (T.sc[:, i:i + 1] for i in range(5))
     v = g.vector
     for b in range(VB):
         v.wait_ge(S["nm%d" % b], 1)
@@ -170,6 +171,7 @@ def rank_program(g, core, T, topo):
         v.wait_ge(S["gq%d" % b], 1)
     v.wait_ge(S.tab, 1)
     v.wait_ge(S.io_c, 1)
+    v.wait_ge(S.arrc, capin)
     v.wait_ge(S.arr, arrive)
     v.tensor_reduce(NM, nms, X, A.min).then_inc(S.v1, 1)
     g.scalar.wait_ge(S.arr, arrive)

@@ -6,26 +6,28 @@ VB, TK, NR = 4, 128, 4
 KINDS = 3
 SLOT = VB * KINDS
 BIG = 2048.0
-Q = 16
-J = 128
+Q = 8
+J = 72
 D = math.log(1.0 + 1.0 / Q)
 _R = 1.0 / (Q * D)
 HALF_GAP = (math.log(_R) - D * Q * (_R - 1.0)) / 2.0
+FREE = 1.0e9
 
 SCRATCH = {
     "hs": ("sbuf", [128, TK], "bfloat16"),
     "ws": ("sbuf", [128, VB * 128], "bfloat16"),
     "ohs": ("sbuf", [128, VB * TK], "bfloat16"),
     "eye": ("sbuf", [128, 128], "bfloat16"),
-    "jt": ("sbuf", [128, J], "float32"),
+    "jt": ("sbuf", [128, 128], "float32"),
     "cap": ("sbuf", [128, J], "float32"),
+    "caps": ("sbuf", [128, J + 1], "float32"),
     "ptab": ("sbuf", [128, J], "float32"),
     "ex": ("sbuf", [128, VB * 128], "float32"),
     "stat": ("sbuf", [128, NR * SLOT], "float32"),
     "fac": ("sbuf", [128, NR * VB], "float32"),
     "fs": ("sbuf", [128, NR * VB], "float32"),
-    "xs": ("sbuf", [128, J], "float32"),
-    "ys": ("sbuf", [128, J], "float32"),
+    "xs": ("sbuf", [128, J + 1], "float32"),
+    "ys": ("sbuf", [128, J + 1], "float32"),
     "sc": ("sbuf", [128, 8], "float32"),
     "pidx": ("sbuf", [128, 1], "float32"),
 }
@@ -33,8 +35,8 @@ for _b in range(VB):
     SCRATCH["za%d" % _b] = ("psum", [128, 512], "float32")
     SCRATCH["zb%d" % _b] = ("psum", [128, 512], "float32")
 
-SEMAPHORES = ["ld_h", "ld_w", "ld_oh", "io_p", "io_j", "diag", "io_c", "tab", "arr", "arrc", "sent",
-              "v1", "e1", "v2", "v3", "v4", "v5", "vg1", "vg2", "v6", "stored"]
+SEMAPHORES = ["ld_h", "ld_w0", "ld_w1", "ld_oh", "io_p", "io_j", "diag", "io_c", "tab", "arr", "arrc", "sent",
+              "fill", "cs", "v1", "e1", "v2", "v3", "v4", "v5", "vg1", "sb1", "sb2", "stored"]
 for _b in range(VB):
     SEMAPHORES += ["za%d" % _b, "zb%d" % _b, "nm%d" % _b, "sm%d" % _b, "gq%d" % _b]
 
@@ -85,9 +87,11 @@ def rank_program(g, core, T, topo):
     S = T.sem
     X = AxisListType.X
     EXP = ActivationFunctionType.Exp
+    IDN = ActivationFunctionType.Identity
     A = AluOpType
     base = rank * SLOT
     stat = T.stat
+    HW = VB * 128 // 2
 
     def col(b, k):
         c = base + KINDS * b + k
@@ -96,15 +100,16 @@ def rank_program(g, core, T, topo):
     def blk(t, b):
         return t[:, 128 * b:128 * b + 128]
 
-    g.sync.dma_start(T.ws[:], T.w[:]).then_inc(S.ld_w, 16)
+    g.sync.dma_start(T.ws[:, 0:HW], T.w[:, 0:HW]).then_inc(S.ld_w0, 16)
     g.scalar.dma_start(T.hs[:], T.h[:]).then_inc(S.ld_h, 16)
+    g.sync.dma_start(T.ws[:, HW:2 * HW], T.w[:, HW:2 * HW]).then_inc(S.ld_w1, 16)
     g.sync.dma_start(T.ohs[:], T.oh[:]).then_inc(S.ld_oh, 16)
 
     home = [c for c in T.cores if topo.chip(c) == topo.chip(core)]
     W = J // len(home)
     k0 = home.index(core)
     mine = T.cap[:, k0 * W:k0 * W + W]
-    g.iota(T.jt[:], [[1, J]], 0, 0, allow_small_or_imprecise_dtypes=True).then_inc(S.io_j, 1)
+    g.iota(T.jt[:], [[1, 128]], 0, 0, allow_small_or_imprecise_dtypes=True).then_inc(S.io_j, 1)
     g.iota(T.pidx[:], [[0, 1]], 0, 1, allow_small_or_imprecise_dtypes=True).then_inc(S.io_p, 1)
     g.iota(mine, [[Q + 1, W]], (Q + 1) * (1 + k0 * W) - J * Q, 0,
            allow_small_or_imprecise_dtypes=True).then_inc(S.io_c, 1)
@@ -118,17 +123,20 @@ def rank_program(g, core, T, topo):
             sent += _count(topo.mask(core, c))
             capin += _count(topo.mask(c, core))
     g.scalar.wait_ge(S.io_j, 1)
-    g.scalar.activation(T.ptab[:], T.jt[:], EXP, bias=math.log(Q) + HALF_GAP, scale=-D).then_inc(S.tab, 1)
+    g.scalar.activation(T.ptab[:], T.jt[:, 0:J], EXP, bias=math.log(Q * D) + HALF_GAP, scale=-D).then_inc(S.tab, 1)
+    g.vector.memset(T.caps[:, J:J + 1], FREE).then_inc(S.fill, 1)
     g.vector.wait_ge(S.io_j, 1)
     g.vector.wait_ge(S.io_p, 1)
-    g.vector.tensor_scalar(T.eye[:], T.jt[:, 0:128], T.pidx[:], BIG, A.is_equal, A.mult).then_inc(S.diag, 1)
+    g.vector.tensor_scalar(T.eye[:], T.jt[:], T.pidx[:], BIG, A.is_equal, A.mult).then_inc(S.diag, 1)
 
     g.tensor.wait_ge(S.ld_h, 16)
-    g.tensor.wait_ge(S.ld_w, 16)
-    for b in range(VB):
-        g.tensor.matmul(T["za%d" % b][:, 0:128], T.hs[:], blk(T.ws, b), True, True).then_inc(S["za%d" % b], 1)
-    for b in range(VB):
-        g.tensor.matmul(T["zb%d" % b][:, 0:128], T.hs[:], blk(T.ws, b), True, False)
+    for half in range(2):
+        g.tensor.wait_ge(S["ld_w%d" % half], 16)
+        bs = range(half * VB // 2, (half + 1) * VB // 2)
+        for b in bs:
+            g.tensor.matmul(T["za%d" % b][:, 0:128], T.hs[:], blk(T.ws, b), True, True).then_inc(S["za%d" % b], 1)
+        for b in bs:
+            g.tensor.matmul(T["zb%d" % b][:, 0:128], T.hs[:], blk(T.ws, b), True, False)
     g.tensor.wait_ge(S.ld_oh, 16)
     g.tensor.wait_ge(S.diag, 1)
     for b in range(VB):
@@ -163,37 +171,40 @@ def rank_program(g, core, T, topo):
     nms = stat[:, 0:NR * SLOT:KINDS]
     sms = stat[:, 1:NR * SLOT:KINDS]
     gqs = stat[:, 2:NR * SLOT:KINDS]
-    NM, SS, NG, BB, LL = (T.sc[:, i:i + 1] for i in range(5))
+    NM, SS, NG, B1 = (T.sc[:, i:i + 1] for i in range(4))
     v = g.vector
+    s = g.scalar
+    v.wait_ge(S.io_c, 1)
+    v.wait_ge(S.arrc, capin)
+    v.tensor_scalar(T.caps[:, 0:J], T.cap[:], D, None, A.mult).then_inc(S.cs, 1)
     for b in range(VB):
         v.wait_ge(S["nm%d" % b], 1)
         v.wait_ge(S["sm%d" % b], 1)
         v.wait_ge(S["gq%d" % b], 1)
     v.wait_ge(S.tab, 1)
-    v.wait_ge(S.io_c, 1)
-    v.wait_ge(S.arrc, capin)
+    v.wait_ge(S.fill, 1)
+    v.wait_ge(S.cs, 1)
     v.wait_ge(S.arr, arrive)
     v.tensor_reduce(NM, nms, X, A.min).then_inc(S.v1, 1)
-    g.scalar.wait_ge(S.arr, arrive)
-    g.scalar.wait_ge(S.v1, 1)
-    g.scalar.activation(T.fac[:], nms, EXP, bias=NM, scale=-1.0).then_inc(S.e1, 1)
+    s.wait_ge(S.arr, arrive)
+    s.wait_ge(S.v1, 1)
+    s.activation(T.fac[:], nms, EXP, bias=NM, scale=-1.0).then_inc(S.e1, 1)
     v.tensor_reduce(NG, gqs, X, A.max, negate=True).then_inc(S.vg1, 1)
-    v.wait_ge(S.v1, 1)
-    v.wait_ge(S.vg1, 1)
-    v.tensor_scalar(BB, NG, BIG, NM, A.add, A.subtract).then_inc(S.vg2, 1)
+    s.wait_ge(S.vg1, 1)
+    s.activation(B1, NG, IDN, bias=BIG, scale=1.0).then_inc(S.sb1, 1)
+    s.wait_ge(S.sb1, 1)
+    s.activation(T.xs[:, J:J + 1], NM, IDN, bias=B1, scale=-1.0).then_inc(S.sb2, 1)
     v.wait_ge(S.e1, 1)
     v.tensor_tensor(T.fs[:], T.fac[:], sms, A.mult).then_inc(S.v2, 1)
     v.wait_ge(S.v2, 1)
     v.tensor_reduce(SS, T.fs[:], X, A.add).then_inc(S.v3, 1)
     v.wait_ge(S.v3, 1)
-    v.tensor_scalar(T.xs[:], T.ptab[:], SS, float(Q), A.mult, A.max).then_inc(S.v4, 1)
+    v.tensor_scalar(T.xs[:, 0:J], T.ptab[:], SS, D * Q, A.mult, A.max).then_inc(S.v4, 1)
+    v.wait_ge(S.sb2, 1)
     v.wait_ge(S.v4, 1)
-    v.tensor_tensor_scan(T.ys[:], T.xs[:], T.cap[:], float(-J * Q), A.add, A.min).then_inc(S.v5, 1)
-    v.wait_ge(S.v5, 1)
-    v.wait_ge(S.vg2, 1)
-    v.tensor_scalar(LL, T.ys[:, J - 1:J], D, BB, A.mult, A.add).then_inc(S.v6, 1)
+    v.tensor_tensor_scan(T.ys[:], T.xs[:], T.caps[:], -D * J * Q, A.add, A.min).then_inc(S.v5, 1)
 
-    g.sync.wait_ge(S.v6, 1)
-    g.sync.dma_start(T.l[:], LL).then_inc(S.stored, 16)
+    g.sync.wait_ge(S.v5, 1)
+    g.sync.dma_start(T.l[:], T.ys[:, J:J + 1]).then_inc(S.stored, 16)
     g.sync.wait_ge(S.stored, 16)
     g.wait_ge(S.sent, sent)

import math
from concourse.bass import DstId, RemoteDMATransfer
from concourse.mybir import AluOpType, AxisListType, ActivationFunctionType

VB, TK, NR = 4, 128, 4
KINDS = 3
SLOT = VB * KINDS
BIG = 2048.0
Q = 8
J = 72
D = math.log(1.0 + 1.0 / Q)
_R = 1.0 / (Q * D)
HALF_GAP = (math.log(_R) - D * Q * (_R - 1.0)) / 2.0
FREE = 1.0e9

SCRATCH = {
    "hs": ("sbuf", [128, TK], "bfloat16"),
    "ws": ("sbuf", [128, VB * 128], "bfloat16"),
    "ohs": ("sbuf", [128, VB * TK], "bfloat16"),
    "eye": ("sbuf", [128, 128], "bfloat16"),
    "jt": ("sbuf", [128, 128], "float32"),
    "cap": ("sbuf", [128, J], "float32"),
    "caps": ("sbuf", [128, J + 1], "float32"),
    "ptab": ("sbuf", [128, J], "float32"),
    "ex": ("sbuf", [128, VB * 128], "float32"),
    "stat": ("sbuf", [128, NR * SLOT], "float32"),
    "fac": ("sbuf", [128, NR * VB], "float32"),
    "fs": ("sbuf", [128, NR * VB], "float32"),
    "xs": ("sbuf", [128, J + 1], "float32"),
    "ys": ("sbuf", [128, J + 1], "float32"),
    "sc": ("sbuf", [128, 8], "float32"),
    "pidx": ("sbuf", [128, 1], "float32"),
}
for _b in range(VB):
    SCRATCH["za%d" % _b] = ("psum", [128, 512], "float32")
    SCRATCH["zb%d" % _b] = ("psum", [128, 512], "float32")

SEMAPHORES = ["ld_h", "ld_w0", "ld_w1", "ld_oh", "io_p", "io_j", "diag", "io_c", "tab", "arr", "arrc", "sent",
              "fill", "cs", "v1", "e1", "v2", "v3", "v4", "v5", "vg1", "sb1", "sb2", "stored"]
for _b in range(VB):
    SEMAPHORES += ["za%d" % _b, "zb%d" % _b, "nm%d" % _b, "sm%d" % _b, "gq%d" % _b]


def _bits(mask):
    return [1 << i for i in range(mask.bit_length()) if (mask >> i) & 1]


def _join(bits):
    m = 0
    for x in bits:
        m |= x
    return m


def _pow2(n):
    p = 1
    while p * 2 <= n:
        p *= 2
    return p


def _plan(core, cores, topo):
    peers = [c for c in cores if c != core]
    near = [c for c in peers if topo.chip(c) == topo.chip(core)]
    far = [c for c in peers if topo.chip(c) != topo.chip(core)]
    leave = topo.mask(core, far[0])
    for c in far:
        leave &= topo.mask(core, c)
    lb = _bits(leave)
    n = _pow2(len(lb) // len(far))
    plan = {c: _join(lb[i * n:(i + 1) * n]) for i, c in enumerate(far)}
    stay = _bits(topo.mask(core, near[0]) & ~leave)
    n = _pow2(len(stay) // len(near))
    for i, c in enumerate(near):
        plan[c] = _join(stay[i * n:(i + 1) * n])
    return plan


def _count(mask):
    return len(_bits(mask))


def rank_program(g, core, T, topo):
    rank = T.rank_of(core)
    if rank is None:
        return
    S = T.sem
    X = AxisListType.X
    EXP = ActivationFunctionType.Exp
    IDN = ActivationFunctionType.Identity
    A = AluOpType
    base = rank * SLOT
    stat = T.stat
    HW = VB * 128 // 2

    def col(b, k):
        c = base + KINDS * b + k
        return stat[:, c:c + 1]

    def blk(t, b):
        return t[:, 128 * b:128 * b + 128]

    g.sync.dma_start(T.ws[:, 0:HW], T.w[:, 0:HW]).then_inc(S.ld_w0, 16)
    g.scalar.dma_start(T.hs[:], T.h[:]).then_inc(S.ld_h, 16)
    g.sync.dma_start(T.ws[:, HW:2 * HW], T.w[:, HW:2 * HW]).then_inc(S.ld_w1, 16)
    g.sync.dma_start(T.ohs[:], T.oh[:]).then_inc(S.ld_oh, 16)

    home = [c for c in T.cores if topo.chip(c) == topo.chip(core)]
    W = J // len(home)
    k0 = home.index(core)
    mine = T.cap[:, k0 * W:k0 * W + W]
    g.iota(T.jt[:], [[1, 128]], 0, 0, allow_small_or_imprecise_dtypes=True).then_inc(S.io_j, 1)
    g.iota(T.pidx[:], [[0, 1]], 0, 1, allow_small_or_imprecise_dtypes=True).then_inc(S.io_p, 1)
    g.iota(mine, [[Q + 1, W]], (Q + 1) * (1 + k0 * W) - J * Q, 0,
           allow_small_or_imprecise_dtypes=True).then_inc(S.io_c, 1)
    g.wait_ge(S.io_c, 1)
    sent = 0
    capin = 0
    for c in home:
        if c != core:
            rid, pid, _ = topo.addr(c)
            g.remote_dma(mine, mine, S.arrc, S.sent, pid, rid, topo.mask(core, c))
            sent += _count(topo.mask(core, c))
            capin += _count(topo.mask(c, core))
    g.scalar.wait_ge(S.io_j, 1)
    g.scalar.activation(T.ptab[:], T.jt[:, 0:J], EXP, bias=math.log(Q * D) + HALF_GAP, scale=-D).then_inc(S.tab, 1)
    g.vector.memset(T.caps[:, J:J + 1], FREE).then_inc(S.fill, 1)
    g.vector.wait_ge(S.io_j, 1)
    g.vector.wait_ge(S.io_p, 1)
    g.vector.tensor_scalar(T.eye[:], T.jt[:], T.pidx[:], BIG, A.is_equal, A.mult).then_inc(S.diag, 1)

    g.tensor.wait_ge(S.ld_h, 16)
    for half in range(2):
        g.tensor.wait_ge(S["ld_w%d" % half], 16)
        bs = range(half * VB // 2, (half + 1) * VB // 2)
        for b in bs:
            g.tensor.matmul(T["za%d" % b][:, 0:128], T.hs[:], blk(T.ws, b), True, True).then_inc(S["za%d" % b], 1)
        for b in bs:
            g.tensor.matmul(T["zb%d" % b][:, 0:128], T.hs[:], blk(T.ws, b), True, False)
    g.tensor.wait_ge(S.ld_oh, 16)
    g.tensor.wait_ge(S.diag, 1)
    for b in range(VB):
        g.tensor.matmul(T["zb%d" % b][:, 0:128], blk(T.ohs, b), T.eye[:], False, True).then_inc(S["zb%d" % b], 1)

    for b in range(VB):
        g.vector.wait_ge(S["za%d" % b], 1)
        g.vector.tensor_reduce(col(b, 0), T["za%d" % b][:, 0:128], X, A.max, negate=True).then_inc(S["nm%d" % b], 1)
        g.scalar.wait_ge(S["nm%d" % b], 1)
        g.scalar.activation(blk(T.ex, b), T["za%d" % b][:, 0:128], EXP, bias=col(b, 0), scale=1.0,
                            accum_out=col(b, 1)).then_inc(S["sm%d" % b], 1)
    for b in range(VB):
        g.vector.wait_ge(S["zb%d" % b], 1)
        g.vector.tensor_reduce(col(b, 2), T["zb%d" % b][:, 0:128], X, A.max).then_inc(S["gq%d" % b], 1)

    plan = _plan(core, T.cores, topo)
    slot = stat[:, base:base + SLOT]
    for b in range(VB):
        g.wait_ge(S["nm%d" % b], 1)
        g.wait_ge(S["sm%d" % b], 1)
    for b in range(VB):
        g.wait_ge(S["gq%d" % b], 1)
    trs = []
    for c in plan:
        rid, pid, _ = topo.addr(c)
        trs.append(RemoteDMATransfer(dst_ids=[DstId(rid=rid, pnc=pid)], dma_engine_mask=plan[c], remote_sem=S.arr,
                                     src=slot, dst=slot))
    g.remote_dma_fused(trs, local_sem=S.sent)
    sent += sum(_count(plan[c]) for c in plan)
    arrive = sum(_count(_plan(c, T.cores, topo)[core]) for c in T.cores if c != core)

    nms = stat[:, 0:NR * SLOT:KINDS]
    sms = stat[:, 1:NR * SLOT:KINDS]
    gqs = stat[:, 2:NR * SLOT:KINDS]
    NM, SS, NG, B1 = (T.sc[:, i:i + 1] for i in range(4))
    v = g.vector
    s = g.scalar
    v.wait_ge(S.io_c, 1)
    v.wait_ge(S.arrc, capin)
    v.tensor_scalar(T.caps[:, 0:J], T.cap[:], D, None, A.mult).then_inc(S.cs, 1)
    for b in range(VB):
        v.wait_ge(S["nm%d" % b], 1)
        v.wait_ge(S["sm%d" % b], 1)
        v.wait_ge(S["gq%d" % b], 1)
    v.wait_ge(S.tab, 1)
    v.wait_ge(S.fill, 1)
    v.wait_ge(S.cs, 1)
    v.wait_ge(S.arr, arrive)
    v.tensor_reduce(NM, nms, X, A.min).then_inc(S.v1, 1)
    s.wait_ge(S.arr, arrive)
    s.wait_ge(S.v1, 1)
    s.activation(T.fac[:], nms, EXP, bias=NM, scale=-1.0).then_inc(S.e1, 1)
    v.tensor_reduce(NG, gqs, X, A.max, negate=True).then_inc(S.vg1, 1)
    s.wait_ge(S.vg1, 1)
    s.activation(B1, NG, IDN, bias=BIG, scale=1.0).then_inc(S.sb1, 1)
    s.wait_ge(S.sb1, 1)
    s.activation(T.xs[:, J:J + 1], NM, IDN, bias=B1, scale=-1.0).then_inc(S.sb2, 1)
    v.wait_ge(S.e1, 1)
    v.tensor_tensor(T.fs[:], T.fac[:], sms, A.mult).then_inc(S.v2, 1)
    v.wait_ge(S.v2, 1)
    v.tensor_reduce(SS, T.fs[:], X, A.add).then_inc(S.v3, 1)
    v.wait_ge(S.v3, 1)
    v.tensor_scalar(T.xs[:, 0:J], T.ptab[:], SS, D * Q, A.mult, A.max).then_inc(S.v4, 1)
    v.wait_ge(S.sb2, 1)
    v.wait_ge(S.v4, 1)
    v.tensor_tensor_scan(T.ys[:], T.xs[:], T.caps[:], -D * J * Q, A.add, A.min).then_inc(S.v5, 1)

    g.sync.wait_ge(S.v5, 1)
    g.sync.dma_start(T.l[:], T.ys[:, J:J + 1]).then_inc(S.stored, 16)
    g.sync.wait_ge(S.stored, 16)
    g.wait_ge(S.sent, sent)
